import numpy as np
import ml_dtypes

BF16 = ml_dtypes.bfloat16


def bf(x):
    return np.asarray(x, np.float32).astype(BF16)


def f32(x):
    return np.asarray(x, np.float32)


def f64(x):
    return np.asarray(x).astype(np.float64)


def striped(idx):
    return np.tile(idx.reshape(-1, 16).T, (8, 1))


def rows(idx, k):
    return np.tile(idx, (k, 1))


def look(tab, idx):
    return np.take_along_axis(f64(tab), rows(idx, len(tab)), axis=1)


K, S, H, D, V, N, M = 128, 2048, 256, 2, 512, 1024, 256


def setup_inputs():
    return {"z": bf(np.random.standard_normal((H, S))), "wt": bf(np.random.standard_normal((H, K)) / np.sqrt(H)), "u0": f32(np.random.uniform(0.2, 1.0, (K, V))), "u1": f32(np.random.uniform(0.2, 1.0, (K, V))), "w": bf(np.random.standard_normal((K, M)) / np.sqrt(K)), "b": f32(0.5 * np.random.standard_normal((M, 1))), "offs": striped(np.random.permutation(S)[:N])}


def reference(z, wt, u0, u1, w, b, offs):
    idx = offs[:16].T.reshape(-1)
    tab = f64(wt).T @ f64(z)
    x = f64(u0) * look(tab, idx[:V]) + f64(u1) * look(tab, idx[1 * V:2 * V])
    return np.maximum(f64(w).T @ x + f64(b), 0.0)

@@ -1,0 +1,75 @@
+import concourse.mybir as mybir
+
+BF16, F32, U16 = mybir.dt.bfloat16, mybir.dt.float32, mybir.dt.uint16
+ADD, MULT, MAX = mybir.AluOpType.add, mybir.AluOpType.mult, mybir.AluOpType.max
+RELU = mybir.ActivationFunctionType.Relu
+
+P = 128
+H = 256
+S = 2048
+V = 512
+M = 256
+BANK = 512
+
+FLOPS = 2 * H * P * S + 3 * P * V + 2 * P * M * V
+
+
+def tile_lookup_pjmix_relu_kernel(tc, z, wt, u0, u1, w, b, offs, out):
+    nc = tc.nc
+    k_blocks, m_blocks = H // P, M // P
+    with (
+        tc.tile_pool(name="held", bufs=1) as held,
+        tc.psum_pool(name="psum", bufs=4) as psum,
+    ):
+        offsets = held.tile([P, 2 * V // 16], U16, name="offsets")
+        nc.sync.dma_start(offsets[:], offs)
+
+        wt_sb = held.tile([P, k_blocks, P], BF16, name="wt_sb")
+        nc.scalar.dma_start(wt_sb[:], wt.rearrange("(t p) r -> p t r", p=P))
+        z_blocked = z.rearrange("(t p) i -> p t i", p=P)
+        z_sb = []
+        for c in range(S // BANK):
+            z_c = held.tile([P, k_blocks, BANK], BF16, name=f"z_{c}")
+            queue = nc.sync if c % 2 == 0 else nc.scalar
+            queue.dma_start(z_c[:], z_blocked[:, :, c * BANK : (c + 1) * BANK])
+            z_sb.append(z_c)
+
+        u0_sb = held.tile([P, V], F32, name="u0_sb")
+        nc.sync.dma_start(u0_sb[:], u0)
+        u1_sb = held.tile([P, V], F32, name="u1_sb")
+        nc.scalar.dma_start(u1_sb[:], u1)
+        w_sb = held.tile([P, M], BF16, name="w_sb")
+        nc.sync.dma_start(w_sb[:], w)
+        b_sb = held.tile([P, m_blocks], F32, name="b_sb")
+        nc.sync.dma_start(b_sb[:], b.rearrange("(m p) o -> p (m o)", p=P))
+
+        tab = held.tile([P, S], F32, name="tab")
+        for c in range(S // BANK):
+            projected = psum.tile([P, BANK], F32, name="projected")
+            for t in range(k_blocks):
+                nc.tensor.matmul(
+                    projected[:], wt_sb[:, t, :], z_sb[c][:, t, :], start=t == 0, stop=t == k_blocks - 1
+                )
+            columns = tab[:, c * BANK : (c + 1) * BANK]
+            if c % 2 == 0:
+                nc.vector.tensor_copy(columns, projected[:])
+            else:
+                nc.scalar.copy(columns, projected[:])
+
+        part0 = held.tile([P, V], F32, name="part0")
+        nc.vector.tensor_tensor(part0[:], tab[:].indirect(offsets[:, 0 : V // 16]), u0_sb[:], MULT)
+        part1 = held.tile([P, V], F32, name="part1")
+        nc.vector.tensor_tensor(part1[:], tab[:].indirect(offsets[:, V // 16 : 2 * V // 16]), u1_sb[:], MULT)
+        x = held.tile([P, V], BF16, name="x")
+        nc.vector.tensor_tensor(x[:], part0[:], part1[:], ADD)
+
+        for m in range(m_blocks):
+            layer = psum.tile([P, V], F32, name="layer", bufs=2)
+            nc.tensor.matmul(layer[:], w_sb[:, m * P : (m + 1) * P], x[:], start=True, stop=True)
+            y = held.tile([P, V], F32, name=f"y_{m}")
+            if m % 2 == 0:
+                nc.scalar.activation(y[:], layer[:], RELU, bias=b_sb[:, m : m + 1])
+                nc.scalar.dma_start(out[m * P : (m + 1) * P, :], y[:])
+            else:
+                nc.vector.tensor_scalar(y[:], layer[:], b_sb[:, m : m + 1], 0.0, ADD, MAX)
+                nc.sync.dma_start(out[m * P : (m + 1) * P, :], y[:])

@@ -11,6 +11,9 @@ V = 512
 M = 256
 BANK = 512
 
+PIECES = 2
+COLS = V // PIECES
+
 FLOPS = 2 * H * P * S + 3 * P * V + 2 * P * M * V
 
 
@@ -56,20 +59,28 @@ def tile_lookup_pjmix_relu_kernel(tc, z, wt, u0, u1, w, b, offs, out):
             else:
                 nc.scalar.copy(columns, projected[:])
 
-        part0 = held.tile([P, V], F32, name="part0")
-        nc.vector.tensor_tensor(part0[:], tab[:].indirect(offsets[:, 0 : V // 16]), u0_sb[:], MULT)
-        part1 = held.tile([P, V], F32, name="part1")
-        nc.vector.tensor_tensor(part1[:], tab[:].indirect(offsets[:, V // 16 : 2 * V // 16]), u1_sb[:], MULT)
-        x = held.tile([P, V], BF16, name="x")
-        nc.vector.tensor_tensor(x[:], part0[:], part1[:], ADD)
+        for piece in range(PIECES):
+            first = piece * COLS
+            is_last = piece == PIECES - 1
 
-        for m in range(m_blocks):
-            layer = psum.tile([P, V], F32, name="layer", bufs=2)
-            nc.tensor.matmul(layer[:], w_sb[:, m * P : (m + 1) * P], x[:], start=True, stop=True)
-            y = held.tile([P, V], F32, name=f"y_{m}")
-            if m % 2 == 0:
-                nc.scalar.activation(y[:], layer[:], RELU, bias=b_sb[:, m : m + 1])
-                nc.scalar.dma_start(out[m * P : (m + 1) * P, :], y[:])
-            else:
-                nc.vector.tensor_scalar(y[:], layer[:], b_sb[:, m : m + 1], 0.0, ADD, MAX)
-                nc.sync.dma_start(out[m * P : (m + 1) * P, :], y[:])
+            parts = []
+            for d, weights in enumerate((u0_sb, u1_sb)):
+                begin = d * V + first
+                entries = offsets[:, begin // 16 : (begin + COLS) // 16]
+                part = held.tile([P, COLS], F32, name=f"part{d}_{piece}")
+                nc.vector.tensor_tensor(part[:], tab[:].indirect(entries), weights[:, first : first + COLS], MULT)
+                parts.append(part)
+            x = held.tile([P, COLS], BF16, name=f"x_{piece}")
+            nc.vector.tensor_tensor(x[:], parts[0][:], parts[1][:], ADD)
+
+            for m in range(m_blocks):
+                layer = psum.tile([P, COLS], F32, name="layer")
+                nc.tensor.matmul(layer[:], w_sb[:, m * P : (m + 1) * P], x[:], start=True, stop=True)
+                y = held.tile([P, COLS], F32, name=f"y_{piece}_{m}")
+                bias = b_sb[:, m : m + 1]
+                out_block = out[m * P : (m + 1) * P, first : first + COLS]
+                if is_last and m == 1:
+                    nc.vector.tensor_scalar(y[:], layer[:], bias, 0.0, ADD, MAX)
+                else:
+                    nc.scalar.activation(y[:], layer[:], RELU, bias=bias)
+                nc.sync.dma_start(out_block, y[:])

@@ -11,6 +11,7 @@ V = 512
 M = 256
 BANK = 512
 
+CHUNK = 256
 PIECES = 2
 COLS = V // PIECES
 
@@ -22,11 +23,8 @@ def tile_lookup_pjmix_relu_kernel(tc, z, wt, u0, u1, w, b, offs, out):
     k_blocks, m_blocks = H // P, M // P
     with (
         tc.tile_pool(name="held", bufs=1) as held,
-        tc.psum_pool(name="psum", bufs=4) as psum,
+        tc.psum_pool(name="psum", bufs=8) as psum,
     ):
-        offsets = held.tile([P, 2 * V // 16], U16, name="offsets")
-        nc.sync.dma_start(offsets[:], offs)
-
         wt_sb = held.tile([P, k_blocks, P], BF16, name="wt_sb")
         nc.scalar.dma_start(wt_sb[:], wt.rearrange("(t p) r -> p t r", p=P))
         z_blocked = z.rearrange("(t p) i -> p t i", p=P)
@@ -36,6 +34,9 @@ def tile_lookup_pjmix_relu_kernel(tc, z, wt, u0, u1, w, b, offs, out):
             queue = nc.sync if c % 2 == 0 else nc.scalar
             queue.dma_start(z_c[:], z_blocked[:, :, c * BANK : (c + 1) * BANK])
             z_sb.append(z_c)
+
+        offsets = held.tile([P, 2 * V // 16], U16, name="offsets")
+        nc.sync.dma_start(offsets[:], offs)
 
         u0_sb = held.tile([P, V], F32, name="u0_sb")
         nc.sync.dma_start(u0_sb[:], u0)
@@ -47,13 +48,13 @@ def tile_lookup_pjmix_relu_kernel(tc, z, wt, u0, u1, w, b, offs, out):
         nc.sync.dma_start(b_sb[:], b.rearrange("(m p) o -> p (m o)", p=P))
 
         tab = held.tile([P, S], F32, name="tab")
-        for c in range(S // BANK):
-            projected = psum.tile([P, BANK], F32, name="projected")
+        for c in range(S // CHUNK):
+            load, begin = divmod(c * CHUNK, BANK)
+            projected = psum.tile([P, CHUNK], F32, name="projected", tag="bank")
             for t in range(k_blocks):
-                nc.tensor.matmul(
-                    projected[:], wt_sb[:, t, :], z_sb[c][:, t, :], start=t == 0, stop=t == k_blocks - 1
-                )
-            columns = tab[:, c * BANK : (c + 1) * BANK]
+                moving = z_sb[load][:, t, begin : begin + CHUNK]
+                nc.tensor.matmul(projected[:], wt_sb[:, t, :], moving, start=t == 0, stop=t == k_blocks - 1)
+            columns = tab[:, c * CHUNK : (c + 1) * CHUNK]
             if c % 2 == 0:
                 nc.vector.tensor_copy(columns, projected[:])
             else:
@@ -74,7 +75,7 @@ def tile_lookup_pjmix_relu_kernel(tc, z, wt, u0, u1, w, b, offs, out):
             nc.vector.tensor_tensor(x[:], parts[0][:], parts[1][:], ADD)
 
             for m in range(m_blocks):
-                layer = psum.tile([P, COLS], F32, name="layer")
+                layer = psum.tile([P, COLS], F32, name="layer", tag="bank")
                 nc.tensor.matmul(layer[:], w_sb[:, m * P : (m + 1) * P], x[:], start=True, stop=True)
                 y = held.tile([P, COLS], F32, name=f"y_{piece}_{m}")
                 bias = b_sb[:, m : m + 1]

@@ -12,6 +12,7 @@ M = 256
 BANK = 512
 
 CHUNK = 256
+WARM_UPS = 6
 PIECES = 2
 COLS = V // PIECES
 
@@ -25,6 +26,12 @@ def tile_lookup_pjmix_relu_kernel(tc, z, wt, u0, u1, w, b, offs, out):
         tc.tile_pool(name="held", bufs=1) as held,
         tc.psum_pool(name="psum", bufs=8) as psum,
     ):
+        zeros = held.tile([P, BANK], BF16, name="zeros")
+        nc.vector.memset(zeros[:], 0.0)
+        unread = psum.tile([P, BANK], F32, name="unread", tag="bank")
+        for i in range(WARM_UPS):
+            nc.tensor.matmul(unread[:], zeros[:, 0:P], zeros[:], start=True, stop=True)
+
         wt_sb = held.tile([P, k_blocks, P], BF16, name="wt_sb")
         nc.scalar.dma_start(wt_sb[:], wt.rearrange("(t p) r -> p t r", p=P))
         z_blocked = z.rearrange("(t p) i -> p t i", p=P)
@@ -84,4 +91,5 @@ def tile_lookup_pjmix_relu_kernel(tc, z, wt, u0, u1, w, b, offs, out):
                     nc.vector.tensor_scalar(y[:], layer[:], bias, 0.0, ADD, MAX)
                 else:
                     nc.scalar.activation(y[:], layer[:], RELU, bias=bias)
-                nc.sync.dma_start(out_block, y[:])
+                store_queue = nc.scalar if is_last and m == 0 else nc.sync
+                store_queue.dma_start(out_block, y[:])

@@ -8,11 +8,12 @@ P = 128
 H = 256
 S = 2048
 V = 512
+D = 2
 M = 256
 BANK = 512
 
 CHUNK = 256
-WARM_UPS = 6
+WARM_UPS = 3
 PIECES = 2
 COLS = V // PIECES
 
@@ -42,13 +43,16 @@ def tile_lookup_pjmix_relu_kernel(tc, z, wt, u0, u1, w, b, offs, out):
             queue.dma_start(z_c[:], z_blocked[:, :, c * BANK : (c + 1) * BANK])
             z_sb.append(z_c)
 
-        offsets = held.tile([P, 2 * V // 16], U16, name="offsets")
+        offsets = held.tile([P, D * V // 16], U16, name="offsets")
         nc.sync.dma_start(offsets[:], offs)
 
-        u0_sb = held.tile([P, V], F32, name="u0_sb")
-        nc.sync.dma_start(u0_sb[:], u0)
-        u1_sb = held.tile([P, V], F32, name="u1_sb")
-        nc.scalar.dma_start(u1_sb[:], u1)
+        u_sb = {}
+        for piece in range(PIECES):
+            for d, u in enumerate((u0, u1)):
+                u_dp = held.tile([P, COLS], F32, name=f"u{d}_{piece}")
+                queue = nc.sync if d == 0 else nc.scalar
+                queue.dma_start(u_dp[:], u[:, piece * COLS : (piece + 1) * COLS])
+                u_sb[d, piece] = u_dp
         w_sb = held.tile([P, M], BF16, name="w_sb")
         nc.sync.dma_start(w_sb[:], w)
         b_sb = held.tile([P, m_blocks], F32, name="b_sb")
@@ -72,11 +76,11 @@ def tile_lookup_pjmix_relu_kernel(tc, z, wt, u0, u1, w, b, offs, out):
             is_last = piece == PIECES - 1
 
             parts = []
-            for d, weights in enumerate((u0_sb, u1_sb)):
+            for d in range(D):
                 begin = d * V + first
                 entries = offsets[:, begin // 16 : (begin + COLS) // 16]
                 part = held.tile([P, COLS], F32, name=f"part{d}_{piece}")
-                nc.vector.tensor_tensor(part[:], tab[:].indirect(entries), weights[:, first : first + COLS], MULT)
+                nc.vector.tensor_tensor(part[:], tab[:].indirect(entries), u_sb[d, piece][:], MULT)
                 parts.append(part)
             x = held.tile([P, COLS], BF16, name=f"x_{piece}")
             nc.vector.tensor_tensor(x[:], parts[0][:], parts[1][:], ADD)

import concourse.mybir as mybir

BF16, F32, U16 = mybir.dt.bfloat16, mybir.dt.float32, mybir.dt.uint16
ADD, MULT, MAX = mybir.AluOpType.add, mybir.AluOpType.mult, mybir.AluOpType.max
RELU = mybir.ActivationFunctionType.Relu

P = 128
H = 256
S = 2048
V = 512
D = 2
M = 256
BANK = 512

CHUNK = 256
WARM_UPS = 3
PIECES = 2
COLS = V // PIECES

FLOPS = 2 * H * P * S + 3 * P * V + 2 * P * M * V


def tile_lookup_pjmix_relu_kernel(tc, z, wt, u0, u1, w, b, offs, out):
    nc = tc.nc
    k_blocks, m_blocks = H // P, M // P
    with (
        tc.tile_pool(name="held", bufs=1) as held,
        tc.psum_pool(name="psum", bufs=8) as psum,
    ):
        zeros = held.tile([P, BANK], BF16, name="zeros")
        nc.vector.memset(zeros[:], 0.0)
        unread = psum.tile([P, BANK], F32, name="unread", tag="bank")
        for i in range(WARM_UPS):
            nc.tensor.matmul(unread[:], zeros[:, 0:P], zeros[:], start=True, stop=True)

        wt_sb = held.tile([P, k_blocks, P], BF16, name="wt_sb")
        nc.scalar.dma_start(wt_sb[:], wt.rearrange("(t p) r -> p t r", p=P))
        z_blocked = z.rearrange("(t p) i -> p t i", p=P)
        z_sb = []
        for c in range(S // BANK):
            z_c = held.tile([P, k_blocks, BANK], BF16, name=f"z_{c}")
            queue = nc.sync if c % 2 == 0 else nc.scalar
            queue.dma_start(z_c[:], z_blocked[:, :, c * BANK : (c + 1) * BANK])
            z_sb.append(z_c)

        offsets = held.tile([P, D * V // 16], U16, name="offsets")
        nc.sync.dma_start(offsets[:], offs)

        u_sb = {}
        for piece in range(PIECES):
            for d, u in enumerate((u0, u1)):
                u_dp = held.tile([P, COLS], F32, name=f"u{d}_{piece}")
                queue = nc.sync if d == 0 else nc.scalar
                queue.dma_start(u_dp[:], u[:, piece * COLS : (piece + 1) * COLS])
                u_sb[d, piece] = u_dp
        w_sb = held.tile([P, M], BF16, name="w_sb")
        nc.sync.dma_start(w_sb[:], w)
        b_sb = held.tile([P, m_blocks], F32, name="b_sb")
        nc.sync.dma_start(b_sb[:], b.rearrange("(m p) o -> p (m o)", p=P))

        tab = held.tile([P, S], F32, name="tab")
        for c in range(S // CHUNK):
            load, begin = divmod(c * CHUNK, BANK)
            projected = psum.tile([P, CHUNK], F32, name="projected", tag="bank")
            for t in range(k_blocks):
                moving = z_sb[load][:, t, begin : begin + CHUNK]
                nc.tensor.matmul(projected[:], wt_sb[:, t, :], moving, start=t == 0, stop=t == k_blocks - 1)
            columns = tab[:, c * CHUNK : (c + 1) * CHUNK]
            if c % 2 == 0:
                nc.vector.tensor_copy(columns, projected[:])
            else:
                nc.scalar.copy(columns, projected[:])

        for piece in range(PIECES):
            first = piece * COLS
            is_last = piece == PIECES - 1

            parts = []
            for d in range(D):
                begin = d * V + first
                entries = offsets[:, begin // 16 : (begin + COLS) // 16]
                part = held.tile([P, COLS], F32, name=f"part{d}_{piece}")
                nc.vector.tensor_tensor(part[:], tab[:].indirect(entries), u_sb[d, piece][:], MULT)
                parts.append(part)
            x = held.tile([P, COLS], BF16, name=f"x_{piece}")
            nc.vector.tensor_tensor(x[:], parts[0][:], parts[1][:], ADD)

            for m in range(m_blocks):
                layer = psum.tile([P, COLS], F32, name="layer", tag="bank")
                nc.tensor.matmul(layer[:], w_sb[:, m * P : (m + 1) * P], x[:], start=True, stop=True)
                y = held.tile([P, COLS], F32, name=f"y_{piece}_{m}")
                bias = b_sb[:, m : m + 1]
                out_block = out[m * P : (m + 1) * P, first : first + COLS]
                if is_last and m == 1:
                    nc.vector.tensor_scalar(y[:], layer[:], bias, 0.0, ADD, MAX)
                else:
                    nc.scalar.activation(y[:], layer[:], RELU, bias=bias)
                store_queue = nc.scalar if is_last and m == 0 else nc.sync
                store_queue.dma_start(out_block, y[:])
